import numpy as np
import ml_dtypes


def mxq(x, axis, fmt="e4m3"):
    dtype, down = {"e4m3": (ml_dtypes.float8_e4m3fn, 7), "e5m2": (ml_dtypes.float8_e5m2, 14)}[fmt]
    v = np.moveaxis(np.asarray(x, np.float32).astype(ml_dtypes.bfloat16).astype(np.float64), axis, -1)
    blocks = v.reshape(v.shape[:-1] + (-1, 32))
    amax = np.abs(blocks).max(-1, keepdims=True)
    byte = np.maximum(np.where(amax > 0, np.frexp(amax)[1] - 1 + 127, 0) - down, 1)
    scale = np.exp2(byte - 127.0)
    codes = (blocks / scale).astype(np.float32).astype(dtype).astype(np.float64)
    return np.moveaxis((codes * scale).reshape(v.shape), -1, axis)


WIDE = False


def mx_kscale(k):
    if not WIDE:
        return np.ones(k)
    levels = np.array([10, -10, 5, -5, 0])
    if k % 512:
        return np.exp2(np.random.permutation(np.resize(levels, k // 32))).repeat(32)
    a = np.empty((k // 512, 16))
    for p in range(k // 512):
        a[p, :8] = np.random.permutation(np.resize(levels, 8))
        for g in range(8):
            far = levels[np.abs(levels - a[p, g]) >= 10]
            a[p, g + 8] = far[np.random.randint(len(far))]
    return np.exp2(a.ravel()).repeat(32)


def f64(x):
    return np.asarray(x).astype(np.float64)


def striped(idx):
    return np.tile(np.asarray(idx).reshape(-1, 16).T, (8, 1)).astype(np.uint16)


def unstriped(offs):
    return offs[:16].T.reshape(-1).astype(np.int64)


def bf(x):
    return np.asarray(x, np.float32).astype(ml_dtypes.bfloat16)


def planes(Y):
    r, m = Y.shape
    b = f64(bf(Y)).reshape(r // 32, 32, m)
    amax = np.abs(b).max(1)
    byte = np.clip(np.where(amax > 0, np.frexp(amax)[1] - 1 + 127 - 7, 1), 1, 254)
    codes = (b * np.exp2(127.0 - byte)[:, None, :]).reshape(r, m).astype(np.float32).astype(ml_dtypes.float8_e4m3fn).view(np.uint8)
    words = codes.reshape(r // 512, 128, 4, m).transpose(0, 1, 3, 2)
    return np.ascontiguousarray(words), np.ascontiguousarray(byte.astype(np.uint8).reshape(r // 512, 16, m))


D, T, I, Q, E = 512, 2048, 512, 256, 512


def setup_inputs():
    n = np.random.standard_normal
    idx = np.random.permutation(T)[:I]
    idx2 = np.random.permutation(T)[:I]
    idx3 = np.random.permutation(T)[:I]
    idx4 = np.random.permutation(Q)[:Q]
    fd = mx_kscale(D)
    fi = mx_kscale(I)
    ti = np.ones(T)
    ti[idx] = fi
    return {
        "query": (n((D, Q)) * 1.0 / np.sqrt(D) * fd[:, None]).astype(np.float32),
        "keys": (n((D, T)) / fd[:, None]).astype(np.float32),
        "os": (np.random.uniform(0.02, 0.08, (1, I)) * fi).astype(np.float32),
        "vals": (n((E, T)) / ti).astype(np.float32),
        "hold": (np.random.uniform(0.3, 1.0, (1, Q))).astype(np.float32),
        "offs": striped(idx),
        "offs2": striped(idx2),
        "offs3": striped(idx3),
        "offs4": striped(idx4),
    }


def reference(query, keys, os, vals, hold, offs, offs2, offs3, offs4):
    idx = unstriped(offs)
    idx2 = unstriped(offs2)
    idx3 = unstriped(offs3)
    idx4 = unstriped(offs4)
    lo3 = np.minimum(f64(keys)[:, idx], f64(keys)[:, idx2])
    hi3 = np.maximum(f64(keys)[:, idx], f64(keys)[:, idx2])
    zk = np.maximum(lo3, np.minimum(hi3, f64(keys)[:, idx3]))
    queryq = mxq(f64(query), 0, "e4m3")
    zkq = mxq(zk, 0, "e4m3")
    s = queryq.T @ zkq
    w = np.maximum(s, 0.0)
    wo1 = w * f64(os)
    wt1 = wo1.T
    vt1 = f64(vals)[:, idx].T
    vt1q = mxq(vt1, 0, "e4m3")
    wt1q = mxq(wt1, 0, "e4m3")
    o = vt1q.T @ wt1q
    y = o - o[:, idx4] * f64(hold)
    words, scales = planes(y)
    return y, words, scales

@@ -1,0 +1,200 @@
+from contextlib import ExitStack
+
+import concourse.mybir as mybir
+from concourse.masks import make_identity
+
+D, T, I, Q, E = 512, 2048, 512, 256, 512
+FLOPS = 2 * D * Q * I + 2 * I * E * Q
+
+F32 = mybir.dt.float32
+BF16 = mybir.dt.bfloat16
+I32 = mybir.dt.int32
+U32 = mybir.dt.uint32
+U16 = mybir.dt.uint16
+U8 = mybir.dt.uint8
+FP8X4 = mybir.dt.float8_e4m3fn_x4
+ALU = mybir.AluOpType
+COPY = mybir.ActivationFunctionType.Copy
+
+P = 128
+PACK = 4
+HALF_Q = Q // 2
+
+
+def tile_attend_keymiddle_comparedrows_lean_pl_kernel(
+    tc, query, keys, slot_factor, vals, hold, offs, offs2, offs3, offs4, out_0, out_1, out_2
+):
+    nc = tc.nc
+    with ExitStack() as ctx:
+        lists = ctx.enter_context(tc.tile_pool(name="lists", bufs=1))
+        sb = ctx.enter_context(tc.tile_pool(name="sb", bufs=1))
+        psum = ctx.enter_context(tc.psum_pool(name="psum", bufs=1))
+
+        list_a = lists.tile([P, I // 16], U16, name="list_a")
+        list_b = lists.tile([P, I // 16], U16, name="list_b")
+        list_c = lists.tile([P, I // 16], U16, name="list_c")
+        list_q = lists.tile([P, Q // 16], U16, name="list_q")
+
+        key_rows = keys.rearrange("(p t) w -> p t w", t=PACK)
+        val_rows = vals.rearrange("(p t) w -> p t w", t=PACK)
+        key_plane = [sb.tile([P, T], F32, name="key_plane%d" % t) for t in range(PACK)]
+        val_plane = [sb.tile([P, T], F32, name="val_plane%d" % t) for t in range(PACK)]
+        query_raw = sb.tile([P, PACK, Q], F32, name="query_raw")
+        factor = sb.tile([P, PACK], F32, name="factor")
+        hold_pairs = sb.tile([P, 2], F32, name="hold_pairs")
+
+        nc.sync.dma_start(key_plane[0][:], key_rows[:, 0, :])
+        nc.sync.dma_start(list_a[:], offs)
+        nc.sync.dma_start(list_b[:], offs2)
+        nc.sync.dma_start(list_c[:], offs3)
+        nc.scalar.dma_start(hold_pairs[:], hold.rearrange("o (p c) -> p (o c)", c=2))
+        nc.scalar.dma_start(factor[:], slot_factor.rearrange("o (p r) -> p (o r)", r=PACK))
+        nc.sync.dma_start(key_plane[1][:], key_rows[:, 1, :])
+        nc.sync.dma_start(query_raw[:], query.rearrange("(p t) w -> p t w", t=PACK))
+        nc.sync.dma_start(key_plane[2][:], key_rows[:, 2, :])
+        nc.sync.dma_start(key_plane[3][:], key_rows[:, 3, :])
+        nc.sync.dma_start(val_plane[0][:], val_rows[:, 0, :])
+        nc.sync.dma_start(list_q[:], offs4)
+        for t in range(1, PACK):
+            nc.sync.dma_start(val_plane[t][:], val_rows[:, t, :])
+
+        identity = sb.tile([P, P], F32, name="identity")
+        make_identity(nc, identity[:])
+
+        hold_bank = psum.tile([P, 2, P], F32, name="hold_bank", tag="turn", bufs=2)
+        for c in range(2):
+            nc.tensor.transpose(hold_bank[:, c, :], hold_pairs[:, c : c + 1].to_broadcast([P, P]), identity[:])
+        hold_rows = sb.tile([P, Q], F32, name="hold_rows")
+        nc.scalar.activation(
+            hold_rows[:].rearrange("p (n c) -> p n c", c=2), hold_bank[:].rearrange("p c n -> p n c"), COPY
+        )
+
+        low = sb.tile([P, PACK, I], F32, name="low")
+        cut = sb.tile([P, PACK, I], F32, name="cut")
+        for t in range(PACK):
+            a = sb.tile([P, I], F32, name="a%d" % t)
+            b = sb.tile([P, I], F32, name="b%d" % t)
+            c = sb.tile([P, I], F32, name="c%d" % t)
+            high = sb.tile([P, I], F32, name="high%d" % t)
+            nc.vector.tensor_copy(a[:], key_plane[t][:].indirect(list_a[:]))
+            nc.scalar.activation(b[:], key_plane[t][:].indirect(list_b[:]), COPY)
+            nc.scalar.activation(c[:], key_plane[t][:].indirect(list_c[:]), COPY)
+            nc.vector.tensor_tensor(high[:], a[:], b[:], ALU.max)
+            nc.vector.tensor_tensor(low[:, t, :], a[:], b[:], ALU.min)
+            nc.vector.tensor_tensor(cut[:, t, :], high[:], c[:], ALU.min)
+
+        query_bf = sb.tile([P, Q, PACK], BF16, name="query_bf", align_bytes=64)
+        nc.scalar.activation(
+            query_bf[:].rearrange("p (c i) t -> p c t i", i=4),
+            query_raw[:].rearrange("p t (c i) -> p c t i", i=4),
+            COPY,
+        )
+        query_codes = sb.tile([P, Q], U32, name="query_codes", align_bytes=64)
+        query_scales = sb.tile([P, Q], U8, name="query_scales", align_bytes=64)
+        nc.vector.quantize_mx(
+            out=query_codes[:].bitcast(FP8X4), scales=query_scales[:], in_=query_bf[:].rearrange("p w t -> p (w t)")
+        )
+
+        low_v = low[:].rearrange("p t (s r) -> p s t r", r=PACK)
+        cut_v = cut[:].rearrange("p t (s r) -> p s t r", r=PACK)
+        key_bf = [sb.tile([P, 2, P, PACK], BF16, name="key_bf%d" % u, align_bytes=64) for u in range(2)]
+        key_codes = [sb.tile([P, 2 * P], U32, name="key_codes%d" % u, align_bytes=64) for u in range(2)]
+        key_scales = [sb.tile([P, 2 * P], U8, name="key_scales%d" % u, align_bytes=64) for u in range(2)]
+        for u in range(2):
+            nc.vector.tensor_tensor(
+                key_bf[u][:].rearrange("p e s t -> p s t e"),
+                low_v[:, :, :, 2 * u : 2 * u + 2],
+                cut_v[:, :, :, 2 * u : 2 * u + 2],
+                ALU.max,
+            )
+        for u in range(2):
+            nc.vector.quantize_mx(
+                out=key_codes[u][:].bitcast(FP8X4),
+                scales=key_scales[u][:],
+                in_=key_bf[u][:].rearrange("p e s t -> p (e s t)"),
+            )
+
+        score_bank = [psum.tile([P, PACK, HALF_Q], F32, name="score_bank%d" % h) for h in range(2)]
+        for u in range(2):
+            for h in range(2):
+                for e in range(2):
+                    cols = slice(e * P, (e + 1) * P)
+                    rows = slice(h * HALF_Q, (h + 1) * HALF_Q)
+                    nc.tensor.matmul_mx(
+                        out=score_bank[h][:, 2 * u + e, :],
+                        lhsT=key_codes[u][:, cols].bitcast(FP8X4),
+                        lhsT_scale=key_scales[u][:, cols],
+                        rhs=query_codes[:, rows].bitcast(FP8X4),
+                        rhs_scale=query_scales[:, rows],
+                        start=True,
+                        stop=True,
+                    )
+        weight_bf = [sb.tile([P, HALF_Q, PACK], BF16, name="weight_bf%d" % h, align_bytes=64) for h in range(2)]
+        weight_codes = sb.tile([P, Q], U32, name="weight_codes", align_bytes=64)
+        weight_scales = sb.tile([P, Q], U8, name="weight_scales", align_bytes=64)
+        for h in range(2):
+            nc.vector.scalar_tensor_tensor(
+                out=weight_bf[h][:],
+                in0=score_bank[h][:].rearrange("p r q -> p q r"),
+                scalar=0.0,
+                in1=factor[:].unsqueeze(1).to_broadcast([P, HALF_Q, PACK]),
+                op0=ALU.max,
+                op1=ALU.mult,
+            )
+        for h in range(2):
+            rows = slice(h * HALF_Q, (h + 1) * HALF_Q)
+            nc.vector.quantize_mx(
+                out=weight_codes[:, rows].bitcast(FP8X4),
+                scales=weight_scales[:, rows],
+                in_=weight_bf[h][:].rearrange("p q r -> p (q r)"),
+            )
+
+        result = sb.tile([P, PACK, Q], F32, name="result")
+        out_rows = out_0.rearrange("(p t) q -> p t q", t=PACK)
+        for t in range(PACK):
+            picked = sb.tile([P, I], BF16, name="picked%d" % t)
+            nc.scalar.activation(picked[:], val_plane[t][:].indirect(list_a[:]), COPY)
+            words = picked[:].bitcast(F32)
+            turn_bank = psum.tile([P, 2, P], F32, name="turn_bank%d" % t, tag="turn", bufs=2)
+            for u in range(2):
+                nc.tensor.transpose(turn_bank[:, u, :], words[:, u : 2 * P : 2], identity[:])
+            value_bf = sb.tile([P, P * PACK], BF16, name="value_bf%d" % t, align_bytes=64)
+            nc.scalar.copy(
+                value_bf[:].bitcast(F32).rearrange("p (n u) -> p n u", u=2), turn_bank[:].rearrange("p u n -> p n u")
+            )
+            value_codes = sb.tile([P, P], U32, name="value_codes%d" % t, align_bytes=64)
+            value_scales = sb.tile([P, P], U8, name="value_scales%d" % t, align_bytes=64)
+            nc.vector.quantize_mx(out=value_codes[:].bitcast(FP8X4), scales=value_scales[:], in_=value_bf[:])
+            sum_bank = psum.tile([P, Q], F32, name="sum_bank%d" % t)
+            nc.tensor.matmul_mx(
+                out=sum_bank[:],
+                lhsT=value_codes[:].bitcast(FP8X4),
+                lhsT_scale=value_scales[:],
+                rhs=weight_codes[:].bitcast(FP8X4),
+                rhs_scale=weight_scales[:],
+                start=True,
+                stop=True,
+            )
+            sums = sb.tile([P, Q], F32, name="sums%d" % t)
+            nc.scalar.activation(sums[:], sum_bank[:], COPY)
+            taken = sb.tile([P, Q], F32, name="taken%d" % t)
+            for h in range(2):
+                rows = slice(h * HALF_Q, (h + 1) * HALF_Q)
+                offsets = list_q[:, h * HALF_Q // 16 : (h + 1) * HALF_Q // 16]
+                nc.vector.tensor_tensor(taken[:, rows], sums[:].indirect(offsets), hold_rows[:, rows], ALU.mult)
+            nc.vector.tensor_tensor(result[:, t, :], sums[:], taken[:], ALU.subtract)
+            nc.sync.dma_start(out_rows[:, t, :], result[:, t, :])
+
+        result_bf = sb.tile([P, Q, PACK], BF16, name="result_bf", align_bytes=64)
+        nc.vector.tensor_copy(
+            result_bf[:].rearrange("p (c i) t -> p c t i", i=4), result[:].rearrange("p t (c i) -> p c t i", i=4)
+        )
+        result_codes = sb.tile([P, Q], U32, name="result_codes", align_bytes=64)
+        result_scales = sb.tile([P, Q], U8, name="result_scales", align_bytes=64)
+        nc.vector.quantize_mx(
+            out=result_codes[:].bitcast(FP8X4), scales=result_scales[:], in_=result_bf[:].rearrange("p w t -> p (w t)")
+        )
+        nc.sync.dma_start(out_1[0].rearrange("p c r -> p (c r)").bitcast(I32), result_codes[:].bitcast(I32))
+        for g in range(4):
+            queue = nc.sync if g % 2 else nc.scalar
+            queue.dma_start(out_2[0, 4 * g : 4 * g + 4, :].bitcast(I32), result_scales[32 * g : 32 * g + 4, :].bitcast(I32))

@@ -19,6 +19,8 @@ COPY = mybir.ActivationFunctionType.Copy
 P = 128
 PACK = 4
 HALF_Q = Q // 2
+PLANE_BYTES = 4 * T
+KIB = 1024
 
 
 def tile_attend_keymiddle_comparedrows_lean_pl_kernel(
@@ -28,6 +30,7 @@ def tile_attend_keymiddle_comparedrows_lean_pl_kernel(
     with ExitStack() as ctx:
         lists = ctx.enter_context(tc.tile_pool(name="lists", bufs=1))
         sb = ctx.enter_context(tc.tile_pool(name="sb", bufs=1))
+        reused = ctx.enter_context(tc.tile_pool(name="reused", bufs=1))
         psum = ctx.enter_context(tc.psum_pool(name="psum", bufs=1))
 
         list_a = lists.tile([P, I // 16], U16, name="list_a")
@@ -38,30 +41,35 @@ def tile_attend_keymiddle_comparedrows_lean_pl_kernel(
         key_rows = keys.rearrange("(p t) w -> p t w", t=PACK)
         val_rows = vals.rearrange("(p t) w -> p t w", t=PACK)
         key_plane = [sb.tile([P, T], F32, name="key_plane%d" % t) for t in range(PACK)]
-        val_plane = [sb.tile([P, T], F32, name="val_plane%d" % t) for t in range(PACK)]
+        val_plane = [sb.tile([P, T], F32, name="val_plane%d" % t) for t in range(1)]
+        val_plane.append(reused.tile([P, T], F32, name="val_plane1", offset=3 * PLANE_BYTES, align_bytes=64))
+        val_plane.append(reused.tile([P, T], F32, name="val_plane2", offset=0, align_bytes=64))
+        val_plane.append(reused.tile([P, T], F32, name="val_plane3", offset=PLANE_BYTES, align_bytes=64))
         query_raw = sb.tile([P, PACK, Q], F32, name="query_raw")
         factor = sb.tile([P, PACK], F32, name="factor")
         hold_pairs = sb.tile([P, 2], F32, name="hold_pairs")
 
+        nc.scalar.dma_start(hold_pairs[:], hold.rearrange("o (p c) -> p (o c)", c=2))
+        nc.scalar.dma_start(factor[:], slot_factor.rearrange("o (p r) -> p (o r)", r=PACK))
         nc.sync.dma_start(key_plane[0][:], key_rows[:, 0, :])
         nc.sync.dma_start(list_a[:], offs)
         nc.sync.dma_start(list_b[:], offs2)
         nc.sync.dma_start(list_c[:], offs3)
-        nc.scalar.dma_start(hold_pairs[:], hold.rearrange("o (p c) -> p (o c)", c=2))
-        nc.scalar.dma_start(factor[:], slot_factor.rearrange("o (p r) -> p (o r)", r=PACK))
-        nc.sync.dma_start(key_plane[1][:], key_rows[:, 1, :])
+        for t in range(1, PACK):
+            nc.sync.dma_start(key_plane[t][:], key_rows[:, t, :])
         nc.sync.dma_start(query_raw[:], query.rearrange("(p t) w -> p t w", t=PACK))
-        nc.sync.dma_start(key_plane[2][:], key_rows[:, 2, :])
-        nc.sync.dma_start(key_plane[3][:], key_rows[:, 3, :])
         nc.sync.dma_start(val_plane[0][:], val_rows[:, 0, :])
         nc.sync.dma_start(list_q[:], offs4)
         for t in range(1, PACK):
             nc.sync.dma_start(val_plane[t][:], val_rows[:, t, :])
 
         identity = sb.tile([P, P], F32, name="identity")
-        make_identity(nc, identity[:])
+        zeros = sb.tile([P, P], BF16, name="zeros")
+        nc.vector.memset(zeros[:], 0.0)
+        nc.scalar.activation(identity[:], zeros[:], COPY)
+        make_identity(nc, identity[:], nomemset=True)
 
-        hold_bank = psum.tile([P, 2, P], F32, name="hold_bank", tag="turn", bufs=2)
+        hold_bank = psum.tile([P, 2, P], F32, name="hold_bank", tag="first")
         for c in range(2):
             nc.tensor.transpose(hold_bank[:, c, :], hold_pairs[:, c : c + 1].to_broadcast([P, P]), identity[:])
         hold_rows = sb.tile([P, Q], F32, name="hold_rows")
@@ -75,10 +83,12 @@ def tile_attend_keymiddle_comparedrows_lean_pl_kernel(
             a = sb.tile([P, I], F32, name="a%d" % t)
             b = sb.tile([P, I], F32, name="b%d" % t)
             c = sb.tile([P, I], F32, name="c%d" % t)
-            high = sb.tile([P, I], F32, name="high%d" % t)
-            nc.vector.tensor_copy(a[:], key_plane[t][:].indirect(list_a[:]))
-            nc.scalar.activation(b[:], key_plane[t][:].indirect(list_b[:]), COPY)
-            nc.scalar.activation(c[:], key_plane[t][:].indirect(list_c[:]), COPY)
+            high = sb.tile([P, I], F32, name="high", bufs=2)
+            for picks, offsets, on_vector in ((a, list_a, t == 0), (b, list_b, False), (c, list_c, t < 3)):
+                if on_vector:
+                    nc.vector.tensor_copy(picks[:], key_plane[t][:].indirect(offsets[:]))
+                else:
+                    nc.scalar.activation(picks[:], key_plane[t][:].indirect(offsets[:]), COPY)
             nc.vector.tensor_tensor(high[:], a[:], b[:], ALU.max)
             nc.vector.tensor_tensor(low[:, t, :], a[:], b[:], ALU.min)
             nc.vector.tensor_tensor(cut[:, t, :], high[:], c[:], ALU.min)
@@ -91,10 +101,6 @@ def tile_attend_keymiddle_comparedrows_lean_pl_kernel(
         )
         query_codes = sb.tile([P, Q], U32, name="query_codes", align_bytes=64)
         query_scales = sb.tile([P, Q], U8, name="query_scales", align_bytes=64)
-        nc.vector.quantize_mx(
-            out=query_codes[:].bitcast(FP8X4), scales=query_scales[:], in_=query_bf[:].rearrange("p w t -> p (w t)")
-        )
-
         low_v = low[:].rearrange("p t (s r) -> p s t r", r=PACK)
         cut_v = cut[:].rearrange("p t (s r) -> p s t r", r=PACK)
         key_bf = [sb.tile([P, 2, P, PACK], BF16, name="key_bf%d" % u, align_bytes=64) for u in range(2)]
@@ -107,7 +113,10 @@ def tile_attend_keymiddle_comparedrows_lean_pl_kernel(
                 cut_v[:, :, :, 2 * u : 2 * u + 2],
                 ALU.max,
             )
-        for u in range(2):
+            if u == 0:
+                nc.vector.quantize_mx(
+                    out=query_codes[:].bitcast(FP8X4), scales=query_scales[:], in_=query_bf[:].rearrange("p w t -> p (w t)")
+                )
             nc.vector.quantize_mx(
                 out=key_codes[u][:].bitcast(FP8X4),
                 scales=key_scales[u][:],
@@ -149,52 +158,114 @@ def tile_attend_keymiddle_comparedrows_lean_pl_kernel(
                 in_=weight_bf[h][:].rearrange("p q r -> p (q r)"),
             )
 
-        result = sb.tile([P, PACK, Q], F32, name="result")
-        out_rows = out_0.rearrange("(p t) q -> p t q", t=PACK)
-        for t in range(PACK):
-            picked = sb.tile([P, I], BF16, name="picked%d" % t)
-            nc.scalar.activation(picked[:], val_plane[t][:].indirect(list_a[:]), COPY)
-            words = picked[:].bitcast(F32)
-            turn_bank = psum.tile([P, 2, P], F32, name="turn_bank%d" % t, tag="turn", bufs=2)
+        picked = [sb.tile([P, I], BF16, name="picked%d" % t) for t in range(PACK)]
+        turn_bank = [
+            psum.tile([P, 2, P], F32, name="turn_bank0", tag="first"),
+            psum.tile([P, 2, P], F32, name="turn_bank1"),
+            None,
+            psum.tile([P, 2, P], F32, name="turn_bank3"),
+        ]
+        both_bank = psum.tile([P, 2, Q], F32, name="both_bank")
+        turn_bank[2] = both_bank[:, 0, :].rearrange("p (u n) -> p u n", u=2)
+        value_bf = [
+            reused.tile([P, I], BF16, name="value_bf0", offset=3 * PLANE_BYTES, align_bytes=64),
+            reused.tile([P, I], BF16, name="value_bf1", offset=0, align_bytes=64),
+            reused.tile([P, I], BF16, name="value_bf2", offset=PLANE_BYTES, align_bytes=64),
+            reused.tile([P, I], BF16, name="value_bf3", offset=2 * PLANE_BYTES, align_bytes=64),
+        ]
+        value_codes = [sb.tile([P, P], U32, name="value_codes%d" % t, align_bytes=64) for t in range(PACK)]
+        value_scales = [sb.tile([P, P], U8, name="value_scales%d" % t, align_bytes=64) for t in range(PACK)]
+
+        def pick_and_turn(t):
+            nc.scalar.activation(picked[t][:], val_plane[t][:].indirect(list_a[:]), COPY)
+            words = picked[t][:].bitcast(F32)
             for u in range(2):
-                nc.tensor.transpose(turn_bank[:, u, :], words[:, u : 2 * P : 2], identity[:])
-            value_bf = sb.tile([P, P * PACK], BF16, name="value_bf%d" % t, align_bytes=64)
+                nc.tensor.transpose(turn_bank[t][:, u, :], words[:, u : 2 * P : 2], identity[:])
+
+        def quantise_values(t):
             nc.scalar.copy(
-                value_bf[:].bitcast(F32).rearrange("p (n u) -> p n u", u=2), turn_bank[:].rearrange("p u n -> p n u")
+                value_bf[t][:].bitcast(F32).rearrange("p (n u) -> p n u", u=2),
+                turn_bank[t][:].rearrange("p u n -> p n u"),
             )
-            value_codes = sb.tile([P, P], U32, name="value_codes%d" % t, align_bytes=64)
-            value_scales = sb.tile([P, P], U8, name="value_scales%d" % t, align_bytes=64)
-            nc.vector.quantize_mx(out=value_codes[:].bitcast(FP8X4), scales=value_scales[:], in_=value_bf[:])
-            sum_bank = psum.tile([P, Q], F32, name="sum_bank%d" % t)
+            nc.vector.quantize_mx(out=value_codes[t][:].bitcast(FP8X4), scales=value_scales[t][:], in_=value_bf[t][:])
+
+        def multiply(t, bank):
             nc.tensor.matmul_mx(
-                out=sum_bank[:],
-                lhsT=value_codes[:].bitcast(FP8X4),
-                lhsT_scale=value_scales[:],
+                out=bank,
+                lhsT=value_codes[t][:].bitcast(FP8X4),
+                lhsT_scale=value_scales[t][:],
                 rhs=weight_codes[:].bitcast(FP8X4),
                 rhs_scale=weight_scales[:],
                 start=True,
                 stop=True,
             )
-            sums = sb.tile([P, Q], F32, name="sums%d" % t)
-            nc.scalar.activation(sums[:], sum_bank[:], COPY)
-            taken = sb.tile([P, Q], F32, name="taken%d" % t)
+
+        halves = [slice(h * HALF_Q, (h + 1) * HALF_Q) for h in range(2)]
+        half_lists = [list_q[:, h * HALF_Q // 16 : (h + 1) * HALF_Q // 16] for h in range(2)]
+        out_rows = out_0.rearrange("(p t) q -> p t q", t=PACK)
+        sums = [
+            sb.tile([P, Q], F32, name="sums0"),
+            reused.tile([P, Q], F32, name="sums1", offset=PLANE_BYTES + KIB, align_bytes=64),
+            sb.tile([P, Q], F32, name="sums2"),
+            sb.tile([P, Q], F32, name="sums3"),
+        ]
+        for t in range(PACK):
+            pick_and_turn(t)
+            if t < 2:
+                quantise_values(t)
+        multiply(0, both_bank[:, 1, :])
+        nc.vector.tensor_copy(sums[0][:], both_bank[:, 1, :])
+        quantise_values(2)
+        sum_bank1 = psum.tile([P, Q], F32, name="sum_bank1", tag="first")
+        multiply(1, sum_bank1[:])
+        nc.scalar.activation(sums[1][:], sum_bank1[:], COPY)
+        quantise_values(3)
+        result = reused.tile([P, PACK, Q], F32, name="result", offset=2 * PLANE_BYTES, align_bytes=64)
+        taken0 = [
+            sb.tile([P, HALF_Q], F32, name="taken0a"),
+            reused.tile([P, HALF_Q], F32, name="taken0b", offset=PLANE_BYTES, align_bytes=64),
+        ]
+        for h in range(2):
+            nc.vector.tensor_tensor(taken0[h][:], sums[0][:].indirect(half_lists[h]), hold_rows[:, halves[h]], ALU.mult)
+        for h in range(2):
+            nc.vector.tensor_tensor(result[:, 0, halves[h]], sums[0][:, halves[h]], taken0[h][:], ALU.subtract)
+        nc.sync.dma_start(out_rows[:, 0, :], result[:, 0, :])
+        taken1 = sb.tile([P, Q], F32, name="taken1")
+        for h in range(2):
+            nc.vector.tensor_tensor(taken1[:, halves[h]], sums[1][:].indirect(half_lists[h]), hold_rows[:, halves[h]], ALU.mult)
+        nc.vector.tensor_tensor(result[:, 1, :], sums[1][:], taken1[:], ALU.subtract)
+        nc.sync.dma_start(out_rows[:, 1, :], result[:, 1, :])
+        for t in range(2, PACK):
+            sum_bank = psum.tile([P, Q], F32, name="sum_bank%d" % t)
+            multiply(t, sum_bank[:])
+            nc.scalar.activation(sums[t][:], sum_bank[:], COPY)
+            named = sb.tile([P, Q], F32, name="named%d" % t)
             for h in range(2):
-                rows = slice(h * HALF_Q, (h + 1) * HALF_Q)
-                offsets = list_q[:, h * HALF_Q // 16 : (h + 1) * HALF_Q // 16]
-                nc.vector.tensor_tensor(taken[:, rows], sums[:].indirect(offsets), hold_rows[:, rows], ALU.mult)
-            nc.vector.tensor_tensor(result[:, t, :], sums[:], taken[:], ALU.subtract)
+                nc.scalar.activation(named[:, halves[h]], sums[t][:].indirect(half_lists[h]), COPY)
+            taken = sb.tile([P, Q], F32, name="taken%d" % t)
+            pieces = halves if t == PACK - 1 else [slice(0, Q)]
+            for rows in pieces:
+                nc.vector.tensor_tensor(taken[:, rows], named[:, rows], hold_rows[:, rows], ALU.mult)
+            for rows in pieces:
+                nc.vector.tensor_tensor(result[:, t, rows], sums[t][:, rows], taken[:, rows], ALU.subtract)
             nc.sync.dma_start(out_rows[:, t, :], result[:, t, :])
 
         result_bf = sb.tile([P, Q, PACK], BF16, name="result_bf", align_bytes=64)
-        nc.vector.tensor_copy(
-            result_bf[:].rearrange("p (c i) t -> p c t i", i=4), result[:].rearrange("p t (c i) -> p c t i", i=4)
-        )
         result_codes = sb.tile([P, Q], U32, name="result_codes", align_bytes=64)
         result_scales = sb.tile([P, Q], U8, name="result_scales", align_bytes=64)
-        nc.vector.quantize_mx(
-            out=result_codes[:].bitcast(FP8X4), scales=result_scales[:], in_=result_bf[:].rearrange("p w t -> p (w t)")
-        )
-        nc.sync.dma_start(out_1[0].rearrange("p c r -> p (c r)").bitcast(I32), result_codes[:].bitcast(I32))
+        for rows in halves:
+            nc.vector.tensor_copy(
+                result_bf[:, rows, :].rearrange("p (c i) t -> p c t i", i=4),
+                result[:, :, rows].rearrange("p t (c i) -> p c t i", i=4),
+            )
+        out_words = out_1[0].rearrange("p c r -> p (c r)").bitcast(I32)
+        for rows in halves:
+            nc.vector.quantize_mx(
+                out=result_codes[:, rows].bitcast(FP8X4),
+                scales=result_scales[:, rows],
+                in_=result_bf[:, rows, :].rearrange("p w t -> p (w t)"),
+            )
+            nc.sync.dma_start(out_words[:, rows], result_codes[:, rows].bitcast(I32))
         for g in range(4):
             queue = nc.sync if g % 2 else nc.scalar
             queue.dma_start(out_2[0, 4 * g : 4 * g + 4, :].bitcast(I32), result_scales[32 * g : 32 * g + 4, :].bitcast(I32))

@@ -41,10 +41,8 @@ def tile_attend_keymiddle_comparedrows_lean_pl_kernel(
         key_rows = keys.rearrange("(p t) w -> p t w", t=PACK)
         val_rows = vals.rearrange("(p t) w -> p t w", t=PACK)
         key_plane = [sb.tile([P, T], F32, name="key_plane%d" % t) for t in range(PACK)]
-        val_plane = [sb.tile([P, T], F32, name="val_plane%d" % t) for t in range(1)]
-        val_plane.append(reused.tile([P, T], F32, name="val_plane1", offset=3 * PLANE_BYTES, align_bytes=64))
-        val_plane.append(reused.tile([P, T], F32, name="val_plane2", offset=0, align_bytes=64))
-        val_plane.append(reused.tile([P, T], F32, name="val_plane3", offset=PLANE_BYTES, align_bytes=64))
+        val_plane = [sb.tile([P, T], F32, name="val_plane%d" % t) for t in range(3)]
+        val_plane.append(reused.tile([P, T], F32, name="val_plane3", offset=0, align_bytes=64))
         query_raw = sb.tile([P, PACK, Q], F32, name="query_raw")
         factor = sb.tile([P, PACK], F32, name="factor")
         hold_pairs = sb.tile([P, 2], F32, name="hold_pairs")
@@ -59,9 +57,9 @@ def tile_attend_keymiddle_comparedrows_lean_pl_kernel(
             nc.sync.dma_start(key_plane[t][:], key_rows[:, t, :])
         nc.sync.dma_start(query_raw[:], query.rearrange("(p t) w -> p t w", t=PACK))
         nc.sync.dma_start(val_plane[0][:], val_rows[:, 0, :])
-        nc.sync.dma_start(list_q[:], offs4)
         for t in range(1, PACK):
             nc.sync.dma_start(val_plane[t][:], val_rows[:, t, :])
+        nc.sync.dma_start(list_q[:], offs4)
 
         identity = sb.tile([P, P], F32, name="identity")
         zeros = sb.tile([P, P], BF16, name="zeros")
@@ -78,7 +76,7 @@ def tile_attend_keymiddle_comparedrows_lean_pl_kernel(
         )
 
         low = sb.tile([P, PACK, I], F32, name="low")
-        cut = sb.tile([P, PACK, I], F32, name="cut")
+        cut = [sb.tile([P, PACK, P, 2], F32, name="cut%d" % u) for u in range(2)]
         for t in range(PACK):
             a = sb.tile([P, I], F32, name="a%d" % t)
             b = sb.tile([P, I], F32, name="b%d" % t)
@@ -91,7 +89,13 @@ def tile_attend_keymiddle_comparedrows_lean_pl_kernel(
                     nc.scalar.activation(picks[:], key_plane[t][:].indirect(offsets[:]), COPY)
             nc.vector.tensor_tensor(high[:], a[:], b[:], ALU.max)
             nc.vector.tensor_tensor(low[:, t, :], a[:], b[:], ALU.min)
-            nc.vector.tensor_tensor(cut[:, t, :], high[:], c[:], ALU.min)
+            for u in range(2):
+                nc.vector.tensor_tensor(
+                    cut[u][:, t],
+                    high[:].rearrange("p (s r) -> p s r", r=PACK)[:, :, 2 * u : 2 * u + 2],
+                    c[:].rearrange("p (s r) -> p s r", r=PACK)[:, :, 2 * u : 2 * u + 2],
+                    ALU.min,
+                )
 
         query_bf = sb.tile([P, Q, PACK], BF16, name="query_bf", align_bytes=64)
         nc.scalar.activation(
@@ -101,44 +105,94 @@ def tile_attend_keymiddle_comparedrows_lean_pl_kernel(
         )
         query_codes = sb.tile([P, Q], U32, name="query_codes", align_bytes=64)
         query_scales = sb.tile([P, Q], U8, name="query_scales", align_bytes=64)
-        low_v = low[:].rearrange("p t (s r) -> p s t r", r=PACK)
-        cut_v = cut[:].rearrange("p t (s r) -> p s t r", r=PACK)
-        key_bf = [sb.tile([P, 2, P, PACK], BF16, name="key_bf%d" % u, align_bytes=64) for u in range(2)]
+        spare = PLANE_BYTES
+        key_bf = [
+            sb.tile([P, 2, P, PACK], BF16, name="key_bf0", align_bytes=64),
+            reused.tile([P, 2, P, PACK], BF16, name="key_bf1", offset=2 * PLANE_BYTES, align_bytes=64),
+        ]
         key_codes = [sb.tile([P, 2 * P], U32, name="key_codes%d" % u, align_bytes=64) for u in range(2)]
         key_scales = [sb.tile([P, 2 * P], U8, name="key_scales%d" % u, align_bytes=64) for u in range(2)]
-        for u in range(2):
+        score_bank = [psum.tile([P, PACK, HALF_Q], F32, name="score_bank%d" % h, tag="score%d" % h) for h in range(2)]
+        picked = [sb.tile([P, I], BF16, name="picked%d" % t) for t in range(PACK)]
+        turn_bank = [
+            score_bank[1][:, 2:4, :],
+            psum.tile([P, 2, P], F32, name="turn_bank1", tag="first"),
+            psum.tile([P, 2, P], F32, name="turn_bank2", tag="turn2"),
+            psum.tile([P, 2, P], F32, name="turn_bank3", tag="turn3"),
+        ]
+        value_bf = [
+            reused.tile([P, I], BF16, name="value_bf0", offset=2 * PLANE_BYTES, align_bytes=64),
+            reused.tile([P, I], BF16, name="value_bf1", offset=spare, align_bytes=64),
+            reused.tile([P, I], BF16, name="value_bf2", offset=0, align_bytes=64),
+            sb.tile([P, I], BF16, name="value_bf3", align_bytes=64),
+        ]
+        value_codes = [sb.tile([P, P], U32, name="value_codes%d" % t, align_bytes=64) for t in range(PACK)]
+        value_scales = [sb.tile([P, P], U8, name="value_scales%d" % t, align_bytes=64) for t in range(PACK)]
+
+        def middle_keys(u):
             nc.vector.tensor_tensor(
                 key_bf[u][:].rearrange("p e s t -> p s t e"),
-                low_v[:, :, :, 2 * u : 2 * u + 2],
-                cut_v[:, :, :, 2 * u : 2 * u + 2],
+                low[:].rearrange("p t (s r) -> p s t r", r=PACK)[:, :, :, 2 * u : 2 * u + 2],
+                cut[u][:].rearrange("p t s e -> p s t e"),
                 ALU.max,
             )
-            if u == 0:
-                nc.vector.quantize_mx(
-                    out=query_codes[:].bitcast(FP8X4), scales=query_scales[:], in_=query_bf[:].rearrange("p w t -> p (w t)")
-                )
+
+        def quantise_keys(u):
             nc.vector.quantize_mx(
                 out=key_codes[u][:].bitcast(FP8X4),
                 scales=key_scales[u][:],
                 in_=key_bf[u][:].rearrange("p e s t -> p (e s t)"),
             )
 
-        score_bank = [psum.tile([P, PACK, HALF_Q], F32, name="score_bank%d" % h) for h in range(2)]
-        for u in range(2):
-            for h in range(2):
-                for e in range(2):
-                    cols = slice(e * P, (e + 1) * P)
-                    rows = slice(h * HALF_Q, (h + 1) * HALF_Q)
-                    nc.tensor.matmul_mx(
-                        out=score_bank[h][:, 2 * u + e, :],
-                        lhsT=key_codes[u][:, cols].bitcast(FP8X4),
-                        lhsT_scale=key_scales[u][:, cols],
-                        rhs=query_codes[:, rows].bitcast(FP8X4),
-                        rhs_scale=query_scales[:, rows],
-                        start=True,
-                        stop=True,
-                    )
-        weight_bf = [sb.tile([P, HALF_Q, PACK], BF16, name="weight_bf%d" % h, align_bytes=64) for h in range(2)]
+        def score(u, h):
+            rows = slice(h * HALF_Q, (h + 1) * HALF_Q)
+            for e in range(2):
+                cols = slice(e * P, (e + 1) * P)
+                nc.tensor.matmul_mx(
+                    out=score_bank[h][:, 2 * u + e, :],
+                    lhsT=key_codes[u][:, cols].bitcast(FP8X4),
+                    lhsT_scale=key_scales[u][:, cols],
+                    rhs=query_codes[:, rows].bitcast(FP8X4),
+                    rhs_scale=query_scales[:, rows],
+                    start=True,
+                    stop=True,
+                )
+
+        def pick_and_turn(t):
+            nc.scalar.activation(picked[t][:], val_plane[t][:].indirect(list_a[:]), COPY)
+            words = picked[t][:].bitcast(F32)
+            for u in range(2):
+                nc.tensor.transpose(turn_bank[t][:, u, :], words[:, u : 2 * P : 2], identity[:])
+
+        def quantise_values(t):
+            move_words = nc.vector.tensor_copy if t < 2 else nc.scalar.copy
+            move_words(
+                value_bf[t][:].bitcast(F32).rearrange("p (n u) -> p n u", u=2),
+                turn_bank[t][:].rearrange("p u n -> p n u"),
+            )
+            nc.vector.quantize_mx(out=value_codes[t][:].bitcast(FP8X4), scales=value_scales[t][:], in_=value_bf[t][:])
+
+        middle_keys(0)
+        nc.vector.quantize_mx(
+            out=query_codes[:].bitcast(FP8X4), scales=query_scales[:], in_=query_bf[:].rearrange("p w t -> p (w t)")
+        )
+        quantise_keys(0)
+        score(0, 0)
+        score(0, 1)
+        pick_and_turn(0)
+        middle_keys(1)
+        quantise_keys(1)
+        score(1, 0)
+        quantise_values(0)
+        score(1, 1)
+        for t in range(1, PACK):
+            pick_and_turn(t)
+
+        halves = [slice(h * HALF_Q, (h + 1) * HALF_Q) for h in range(2)]
+        weight_bf = [
+            sb.tile([P, HALF_Q, PACK], BF16, name="weight_bf0", align_bytes=64),
+            reused.tile([P, HALF_Q, PACK], BF16, name="weight_bf1", offset=spare, align_bytes=64),
+        ]
         weight_codes = sb.tile([P, Q], U32, name="weight_codes", align_bytes=64)
         weight_scales = sb.tile([P, Q], U8, name="weight_scales", align_bytes=64)
         for h in range(2):
@@ -151,47 +205,21 @@ def tile_attend_keymiddle_comparedrows_lean_pl_kernel(
                 op1=ALU.mult,
             )
         for h in range(2):
-            rows = slice(h * HALF_Q, (h + 1) * HALF_Q)
             nc.vector.quantize_mx(
-                out=weight_codes[:, rows].bitcast(FP8X4),
-                scales=weight_scales[:, rows],
+                out=weight_codes[:, halves[h]].bitcast(FP8X4),
+                scales=weight_scales[:, halves[h]],
                 in_=weight_bf[h][:].rearrange("p q r -> p (q r)"),
             )
 
-        picked = [sb.tile([P, I], BF16, name="picked%d" % t) for t in range(PACK)]
-        turn_bank = [
-            psum.tile([P, 2, P], F32, name="turn_bank0", tag="first"),
-            psum.tile([P, 2, P], F32, name="turn_bank1"),
-            None,
-            psum.tile([P, 2, P], F32, name="turn_bank3"),
+        sum_bank = [
+            psum.tile([P, Q], F32, name="sum_bank%d" % t, tag=tag)
+            for t, tag in enumerate(("turn2", "turn3", "score0", "score1"))
         ]
-        both_bank = psum.tile([P, 2, Q], F32, name="both_bank")
-        turn_bank[2] = both_bank[:, 0, :].rearrange("p (u n) -> p u n", u=2)
-        value_bf = [
-            reused.tile([P, I], BF16, name="value_bf0", offset=3 * PLANE_BYTES, align_bytes=64),
-            reused.tile([P, I], BF16, name="value_bf1", offset=0, align_bytes=64),
-            reused.tile([P, I], BF16, name="value_bf2", offset=PLANE_BYTES, align_bytes=64),
-            reused.tile([P, I], BF16, name="value_bf3", offset=2 * PLANE_BYTES, align_bytes=64),
-        ]
-        value_codes = [sb.tile([P, P], U32, name="value_codes%d" % t, align_bytes=64) for t in range(PACK)]
-        value_scales = [sb.tile([P, P], U8, name="value_scales%d" % t, align_bytes=64) for t in range(PACK)]
+        sums = [sb.tile([P, Q], F32, name="sums%d" % t) for t in range(PACK)]
 
-        def pick_and_turn(t):
-            nc.scalar.activation(picked[t][:], val_plane[t][:].indirect(list_a[:]), COPY)
-            words = picked[t][:].bitcast(F32)
-            for u in range(2):
-                nc.tensor.transpose(turn_bank[t][:, u, :], words[:, u : 2 * P : 2], identity[:])
-
-        def quantise_values(t):
-            nc.scalar.copy(
-                value_bf[t][:].bitcast(F32).rearrange("p (n u) -> p n u", u=2),
-                turn_bank[t][:].rearrange("p u n -> p n u"),
-            )
-            nc.vector.quantize_mx(out=value_codes[t][:].bitcast(FP8X4), scales=value_scales[t][:], in_=value_bf[t][:])
-
-        def multiply(t, bank):
+        def add_up(t):
             nc.tensor.matmul_mx(
-                out=bank,
+                out=sum_bank[t][:],
                 lhsT=value_codes[t][:].bitcast(FP8X4),
                 lhsT_scale=value_scales[t][:],
                 rhs=weight_codes[:].bitcast(FP8X4),
@@ -199,64 +227,45 @@ def tile_attend_keymiddle_comparedrows_lean_pl_kernel(
                 start=True,
                 stop=True,
             )
+            nc.scalar.copy(sums[t][:], sum_bank[t][:])
 
-        halves = [slice(h * HALF_Q, (h + 1) * HALF_Q) for h in range(2)]
+        for t in range(1, PACK):
+            quantise_values(t)
+        add_up(0)
+        add_up(1)
+
         half_lists = [list_q[:, h * HALF_Q // 16 : (h + 1) * HALF_Q // 16] for h in range(2)]
         out_rows = out_0.rearrange("(p t) q -> p t q", t=PACK)
-        sums = [
-            sb.tile([P, Q], F32, name="sums0"),
-            reused.tile([P, Q], F32, name="sums1", offset=PLANE_BYTES + KIB, align_bytes=64),
-            sb.tile([P, Q], F32, name="sums2"),
-            sb.tile([P, Q], F32, name="sums3"),
-        ]
+        result = [sb.tile([P, 2, Q], F32, name="result%d" % u) for u in range(2)]
         for t in range(PACK):
-            pick_and_turn(t)
-            if t < 2:
-                quantise_values(t)
-        multiply(0, both_bank[:, 1, :])
-        nc.vector.tensor_copy(sums[0][:], both_bank[:, 1, :])
-        quantise_values(2)
-        sum_bank1 = psum.tile([P, Q], F32, name="sum_bank1", tag="first")
-        multiply(1, sum_bank1[:])
-        nc.scalar.activation(sums[1][:], sum_bank1[:], COPY)
-        quantise_values(3)
-        result = reused.tile([P, PACK, Q], F32, name="result", offset=2 * PLANE_BYTES, align_bytes=64)
-        taken0 = [
-            sb.tile([P, HALF_Q], F32, name="taken0a"),
-            reused.tile([P, HALF_Q], F32, name="taken0b", offset=PLANE_BYTES, align_bytes=64),
-        ]
-        for h in range(2):
-            nc.vector.tensor_tensor(taken0[h][:], sums[0][:].indirect(half_lists[h]), hold_rows[:, halves[h]], ALU.mult)
-        for h in range(2):
-            nc.vector.tensor_tensor(result[:, 0, halves[h]], sums[0][:, halves[h]], taken0[h][:], ALU.subtract)
-        nc.sync.dma_start(out_rows[:, 0, :], result[:, 0, :])
-        taken1 = sb.tile([P, Q], F32, name="taken1")
-        for h in range(2):
-            nc.vector.tensor_tensor(taken1[:, halves[h]], sums[1][:].indirect(half_lists[h]), hold_rows[:, halves[h]], ALU.mult)
-        nc.vector.tensor_tensor(result[:, 1, :], sums[1][:], taken1[:], ALU.subtract)
-        nc.sync.dma_start(out_rows[:, 1, :], result[:, 1, :])
-        for t in range(2, PACK):
-            sum_bank = psum.tile([P, Q], F32, name="sum_bank%d" % t)
-            multiply(t, sum_bank[:])
-            nc.scalar.activation(sums[t][:], sum_bank[:], COPY)
-            named = sb.tile([P, Q], F32, name="named%d" % t)
-            for h in range(2):
-                nc.scalar.activation(named[:, halves[h]], sums[t][:].indirect(half_lists[h]), COPY)
             taken = sb.tile([P, Q], F32, name="taken%d" % t)
-            pieces = halves if t == PACK - 1 else [slice(0, Q)]
-            for rows in pieces:
-                nc.vector.tensor_tensor(taken[:, rows], named[:, rows], hold_rows[:, rows], ALU.mult)
-            for rows in pieces:
-                nc.vector.tensor_tensor(result[:, t, rows], sums[t][:, rows], taken[:, rows], ALU.subtract)
-            nc.sync.dma_start(out_rows[:, t, :], result[:, t, :])
+            if t >= 2:
+                add_up(t)
+            if t in (1, 2):
+                named = sb.tile([P, Q], F32, name="named%d" % t)
+                for h in range(2):
+                    nc.scalar.activation(named[:, halves[h]], sums[t][:].indirect(half_lists[h]), COPY)
+                nc.vector.tensor_tensor(taken[:], named[:], hold_rows[:], ALU.mult)
+            else:
+                for h in range(2):
+                    nc.vector.tensor_tensor(
+                        taken[:, halves[h]], sums[t][:].indirect(half_lists[h]), hold_rows[:, halves[h]], ALU.mult
+                    )
+            for rows in halves if t == PACK - 1 else [slice(0, Q)]:
+                nc.vector.tensor_tensor(result[t // 2][:, t % 2, rows], sums[t][:, rows], taken[:, rows], ALU.subtract)
+            nc.sync.dma_start(out_rows[:, t, :], result[t // 2][:, t % 2, :])
 
         result_bf = sb.tile([P, Q, PACK], BF16, name="result_bf", align_bytes=64)
         result_codes = sb.tile([P, Q], U32, name="result_codes", align_bytes=64)
         result_scales = sb.tile([P, Q], U8, name="result_scales", align_bytes=64)
+        nc.scalar.copy(
+            result_bf[:, :, 0:2].rearrange("p (c i) t -> p c t i", i=4),
+            result[0][:].rearrange("p t (c i) -> p c t i", i=4),
+        )
         for rows in halves:
             nc.vector.tensor_copy(
-                result_bf[:, rows, :].rearrange("p (c i) t -> p c t i", i=4),
-                result[:, :, rows].rearrange("p t (c i) -> p c t i", i=4),
+                result_bf[:, rows, 2:4].rearrange("p (c i) t -> p c t i", i=4),
+                result[1][:, :, rows].rearrange("p t (c i) -> p c t i", i=4),
             )
         out_words = out_1[0].rearrange("p c r -> p (c r)").bitcast(I32)
         for rows in halves:

@@ -20,7 +20,7 @@ P = 128
 PACK = 4
 HALF_Q = Q // 2
 PLANE_BYTES = 4 * T
-KIB = 1024
+THIRD_ON_VECTOR = (256, 512, 512, 256)
 
 
 def tile_attend_keymiddle_comparedrows_lean_pl_kernel(
@@ -82,11 +82,12 @@ def tile_attend_keymiddle_comparedrows_lean_pl_kernel(
             b = sb.tile([P, I], F32, name="b%d" % t)
             c = sb.tile([P, I], F32, name="c%d" % t)
             high = sb.tile([P, I], F32, name="high", bufs=2)
-            for picks, offsets, on_vector in ((a, list_a, t == 0), (b, list_b, False), (c, list_c, t < 3)):
-                if on_vector:
-                    nc.vector.tensor_copy(picks[:], key_plane[t][:].indirect(offsets[:]))
-                else:
-                    nc.scalar.activation(picks[:], key_plane[t][:].indirect(offsets[:]), COPY)
+            shares = ((a, list_a, I if t == 0 else 0), (b, list_b, 0), (c, list_c, THIRD_ON_VECTOR[t]))
+            for picks, offsets, n in shares:
+                if n > 0:
+                    nc.vector.tensor_copy(picks[:, :n], key_plane[t][:].indirect(offsets[:, : n // 16]))
+                if n < I:
+                    nc.scalar.activation(picks[:, n:], key_plane[t][:].indirect(offsets[:, n // 16 :]), COPY)
             nc.vector.tensor_tensor(high[:], a[:], b[:], ALU.max)
             nc.vector.tensor_tensor(low[:, t, :], a[:], b[:], ALU.min)
             for u in range(2):
@@ -231,29 +232,33 @@ def tile_attend_keymiddle_comparedrows_lean_pl_kernel(
 
         for t in range(1, PACK):
             quantise_values(t)
-        add_up(0)
-        add_up(1)
+        for t in range(PACK):
+            add_up(t)
 
         half_lists = [list_q[:, h * HALF_Q // 16 : (h + 1) * HALF_Q // 16] for h in range(2)]
         out_rows = out_0.rearrange("(p t) q -> p t q", t=PACK)
         result = [sb.tile([P, 2, Q], F32, name="result%d" % u) for u in range(2)]
-        for t in range(PACK):
-            taken = sb.tile([P, Q], F32, name="taken%d" % t)
-            if t >= 2:
-                add_up(t)
-            if t in (1, 2):
-                named = sb.tile([P, Q], F32, name="named%d" % t)
-                for h in range(2):
-                    nc.scalar.activation(named[:, halves[h]], sums[t][:].indirect(half_lists[h]), COPY)
-                nc.vector.tensor_tensor(taken[:], named[:], hold_rows[:], ALU.mult)
-            else:
-                for h in range(2):
-                    nc.vector.tensor_tensor(
-                        taken[:, halves[h]], sums[t][:].indirect(half_lists[h]), hold_rows[:, halves[h]], ALU.mult
-                    )
+        taken = [sb.tile([P, Q], F32, name="taken%d" % t, tag="taken", bufs=2) for t in range(PACK)]
+
+        def take_off(t):
             for rows in halves if t == PACK - 1 else [slice(0, Q)]:
-                nc.vector.tensor_tensor(result[t // 2][:, t % 2, rows], sums[t][:, rows], taken[:, rows], ALU.subtract)
+                nc.vector.tensor_tensor(result[t // 2][:, t % 2, rows], sums[t][:, rows], taken[t][:, rows], ALU.subtract)
             nc.sync.dma_start(out_rows[:, t, :], result[t // 2][:, t % 2, :])
+
+        for t in (0, 1):
+            for h in range(2):
+                nc.vector.tensor_tensor(
+                    taken[t][:, halves[h]], sums[t][:].indirect(half_lists[h]), hold_rows[:, halves[h]], ALU.mult
+                )
+        for t in (0, 1):
+            take_off(t)
+        for t in (2, 3):
+            named = sb.tile([P, Q], F32, name="named%d" % t)
+            for h in range(2):
+                nc.scalar.activation(named[:, halves[h]], sums[t][:].indirect(half_lists[h]), COPY)
+            nc.vector.tensor_tensor(taken[t][:], named[:], hold_rows[:], ALU.mult)
+        for t in (2, 3):
+            take_off(t)
 
         result_bf = sb.tile([P, Q, PACK], BF16, name="result_bf", align_bytes=64)
         result_codes = sb.tile([P, Q], U32, name="result_codes", align_bytes=64)

@@ -237,13 +237,13 @@ def tile_attend_keymiddle_comparedrows_lean_pl_kernel(
 
         half_lists = [list_q[:, h * HALF_Q // 16 : (h + 1) * HALF_Q // 16] for h in range(2)]
         out_rows = out_0.rearrange("(p t) q -> p t q", t=PACK)
-        result = [sb.tile([P, 2, Q], F32, name="result%d" % u) for u in range(2)]
+        result = sb.tile([P, PACK, Q], F32, name="result")
         taken = [sb.tile([P, Q], F32, name="taken%d" % t, tag="taken", bufs=2) for t in range(PACK)]
 
         def take_off(t):
             for rows in halves if t == PACK - 1 else [slice(0, Q)]:
-                nc.vector.tensor_tensor(result[t // 2][:, t % 2, rows], sums[t][:, rows], taken[t][:, rows], ALU.subtract)
-            nc.sync.dma_start(out_rows[:, t, :], result[t // 2][:, t % 2, :])
+                nc.vector.tensor_tensor(result[:, t, rows], sums[t][:, rows], taken[t][:, rows], ALU.subtract)
+            nc.sync.dma_start(out_rows[:, t, :], result[:, t, :])
 
         for t in (0, 1):
             for h in range(2):
@@ -263,14 +263,10 @@ def tile_attend_keymiddle_comparedrows_lean_pl_kernel(
         result_bf = sb.tile([P, Q, PACK], BF16, name="result_bf", align_bytes=64)
         result_codes = sb.tile([P, Q], U32, name="result_codes", align_bytes=64)
         result_scales = sb.tile([P, Q], U8, name="result_scales", align_bytes=64)
-        nc.scalar.copy(
-            result_bf[:, :, 0:2].rearrange("p (c i) t -> p c t i", i=4),
-            result[0][:].rearrange("p t (c i) -> p c t i", i=4),
-        )
         for rows in halves:
             nc.vector.tensor_copy(
-                result_bf[:, rows, 2:4].rearrange("p (c i) t -> p c t i", i=4),
-                result[1][:, :, rows].rearrange("p t (c i) -> p c t i", i=4),
+                result_bf[:, rows, :].rearrange("p (c i) t -> p c t i", i=4),
+                result[:, :, rows].rearrange("p t (c i) -> p c t i", i=4),
             )
         out_words = out_1[0].rearrange("p c r -> p (c r)").bitcast(I32)
         for rows in halves:

from contextlib import ExitStack

import concourse.mybir as mybir
from concourse.masks import make_identity

D, T, I, Q, E = 512, 2048, 512, 256, 512
FLOPS = 2 * D * Q * I + 2 * I * E * Q

F32 = mybir.dt.float32
BF16 = mybir.dt.bfloat16
I32 = mybir.dt.int32
U32 = mybir.dt.uint32
U16 = mybir.dt.uint16
U8 = mybir.dt.uint8
FP8X4 = mybir.dt.float8_e4m3fn_x4
ALU = mybir.AluOpType
COPY = mybir.ActivationFunctionType.Copy

P = 128
PACK = 4
HALF_Q = Q // 2
PLANE_BYTES = 4 * T
THIRD_ON_VECTOR = (256, 512, 512, 256)


def tile_attend_keymiddle_comparedrows_lean_pl_kernel(
    tc, query, keys, slot_factor, vals, hold, offs, offs2, offs3, offs4, out_0, out_1, out_2
):
    nc = tc.nc
    with ExitStack() as ctx:
        lists = ctx.enter_context(tc.tile_pool(name="lists", bufs=1))
        sb = ctx.enter_context(tc.tile_pool(name="sb", bufs=1))
        reused = ctx.enter_context(tc.tile_pool(name="reused", bufs=1))
        psum = ctx.enter_context(tc.psum_pool(name="psum", bufs=1))

        list_a = lists.tile([P, I // 16], U16, name="list_a")
        list_b = lists.tile([P, I // 16], U16, name="list_b")
        list_c = lists.tile([P, I // 16], U16, name="list_c")
        list_q = lists.tile([P, Q // 16], U16, name="list_q")

        key_rows = keys.rearrange("(p t) w -> p t w", t=PACK)
        val_rows = vals.rearrange("(p t) w -> p t w", t=PACK)
        key_plane = [sb.tile([P, T], F32, name="key_plane%d" % t) for t in range(PACK)]
        val_plane = [sb.tile([P, T], F32, name="val_plane%d" % t) for t in range(3)]
        val_plane.append(reused.tile([P, T], F32, name="val_plane3", offset=0, align_bytes=64))
        query_raw = sb.tile([P, PACK, Q], F32, name="query_raw")
        factor = sb.tile([P, PACK], F32, name="factor")
        hold_pairs = sb.tile([P, 2], F32, name="hold_pairs")

        nc.scalar.dma_start(hold_pairs[:], hold.rearrange("o (p c) -> p (o c)", c=2))
        nc.scalar.dma_start(factor[:], slot_factor.rearrange("o (p r) -> p (o r)", r=PACK))
        nc.sync.dma_start(key_plane[0][:], key_rows[:, 0, :])
        nc.sync.dma_start(list_a[:], offs)
        nc.sync.dma_start(list_b[:], offs2)
        nc.sync.dma_start(list_c[:], offs3)
        for t in range(1, PACK):
            nc.sync.dma_start(key_plane[t][:], key_rows[:, t, :])
        nc.sync.dma_start(query_raw[:], query.rearrange("(p t) w -> p t w", t=PACK))
        nc.sync.dma_start(val_plane[0][:], val_rows[:, 0, :])
        for t in range(1, PACK):
            nc.sync.dma_start(val_plane[t][:], val_rows[:, t, :])
        nc.sync.dma_start(list_q[:], offs4)

        identity = sb.tile([P, P], F32, name="identity")
        zeros = sb.tile([P, P], BF16, name="zeros")
        nc.vector.memset(zeros[:], 0.0)
        nc.scalar.activation(identity[:], zeros[:], COPY)
        make_identity(nc, identity[:], nomemset=True)

        hold_bank = psum.tile([P, 2, P], F32, name="hold_bank", tag="first")
        for c in range(2):
            nc.tensor.transpose(hold_bank[:, c, :], hold_pairs[:, c : c + 1].to_broadcast([P, P]), identity[:])
        hold_rows = sb.tile([P, Q], F32, name="hold_rows")
        nc.scalar.activation(
            hold_rows[:].rearrange("p (n c) -> p n c", c=2), hold_bank[:].rearrange("p c n -> p n c"), COPY
        )

        low = sb.tile([P, PACK, I], F32, name="low")
        cut = [sb.tile([P, PACK, P, 2], F32, name="cut%d" % u) for u in range(2)]
        for t in range(PACK):
            a = sb.tile([P, I], F32, name="a%d" % t)
            b = sb.tile([P, I], F32, name="b%d" % t)
            c = sb.tile([P, I], F32, name="c%d" % t)
            high = sb.tile([P, I], F32, name="high", bufs=2)
            shares = ((a, list_a, I if t == 0 else 0), (b, list_b, 0), (c, list_c, THIRD_ON_VECTOR[t]))
            for picks, offsets, n in shares:
                if n > 0:
                    nc.vector.tensor_copy(picks[:, :n], key_plane[t][:].indirect(offsets[:, : n // 16]))
                if n < I:
                    nc.scalar.activation(picks[:, n:], key_plane[t][:].indirect(offsets[:, n // 16 :]), COPY)
            nc.vector.tensor_tensor(high[:], a[:], b[:], ALU.max)
            nc.vector.tensor_tensor(low[:, t, :], a[:], b[:], ALU.min)
            for u in range(2):
                nc.vector.tensor_tensor(
                    cut[u][:, t],
                    high[:].rearrange("p (s r) -> p s r", r=PACK)[:, :, 2 * u : 2 * u + 2],
                    c[:].rearrange("p (s r) -> p s r", r=PACK)[:, :, 2 * u : 2 * u + 2],
                    ALU.min,
                )

        query_bf = sb.tile([P, Q, PACK], BF16, name="query_bf", align_bytes=64)
        nc.scalar.activation(
            query_bf[:].rearrange("p (c i) t -> p c t i", i=4),
            query_raw[:].rearrange("p t (c i) -> p c t i", i=4),
            COPY,
        )
        query_codes = sb.tile([P, Q], U32, name="query_codes", align_bytes=64)
        query_scales = sb.tile([P, Q], U8, name="query_scales", align_bytes=64)
        spare = PLANE_BYTES
        key_bf = [
            sb.tile([P, 2, P, PACK], BF16, name="key_bf0", align_bytes=64),
            reused.tile([P, 2, P, PACK], BF16, name="key_bf1", offset=2 * PLANE_BYTES, align_bytes=64),
        ]
        key_codes = [sb.tile([P, 2 * P], U32, name="key_codes%d" % u, align_bytes=64) for u in range(2)]
        key_scales = [sb.tile([P, 2 * P], U8, name="key_scales%d" % u, align_bytes=64) for u in range(2)]
        score_bank = [psum.tile([P, PACK, HALF_Q], F32, name="score_bank%d" % h, tag="score%d" % h) for h in range(2)]
        picked = [sb.tile([P, I], BF16, name="picked%d" % t) for t in range(PACK)]
        turn_bank = [
            score_bank[1][:, 2:4, :],
            psum.tile([P, 2, P], F32, name="turn_bank1", tag="first"),
            psum.tile([P, 2, P], F32, name="turn_bank2", tag="turn2"),
            psum.tile([P, 2, P], F32, name="turn_bank3", tag="turn3"),
        ]
        value_bf = [
            reused.tile([P, I], BF16, name="value_bf0", offset=2 * PLANE_BYTES, align_bytes=64),
            reused.tile([P, I], BF16, name="value_bf1", offset=spare, align_bytes=64),
            reused.tile([P, I], BF16, name="value_bf2", offset=0, align_bytes=64),
            sb.tile([P, I], BF16, name="value_bf3", align_bytes=64),
        ]
        value_codes = [sb.tile([P, P], U32, name="value_codes%d" % t, align_bytes=64) for t in range(PACK)]
        value_scales = [sb.tile([P, P], U8, name="value_scales%d" % t, align_bytes=64) for t in range(PACK)]

        def middle_keys(u):
            nc.vector.tensor_tensor(
                key_bf[u][:].rearrange("p e s t -> p s t e"),
                low[:].rearrange("p t (s r) -> p s t r", r=PACK)[:, :, :, 2 * u : 2 * u + 2],
                cut[u][:].rearrange("p t s e -> p s t e"),
                ALU.max,
            )

        def quantise_keys(u):
            nc.vector.quantize_mx(
                out=key_codes[u][:].bitcast(FP8X4),
                scales=key_scales[u][:],
                in_=key_bf[u][:].rearrange("p e s t -> p (e s t)"),
            )

        def score(u, h):
            rows = slice(h * HALF_Q, (h + 1) * HALF_Q)
            for e in range(2):
                cols = slice(e * P, (e + 1) * P)
                nc.tensor.matmul_mx(
                    out=score_bank[h][:, 2 * u + e, :],
                    lhsT=key_codes[u][:, cols].bitcast(FP8X4),
                    lhsT_scale=key_scales[u][:, cols],
                    rhs=query_codes[:, rows].bitcast(FP8X4),
                    rhs_scale=query_scales[:, rows],
                    start=True,
                    stop=True,
                )

        def pick_and_turn(t):
            nc.scalar.activation(picked[t][:], val_plane[t][:].indirect(list_a[:]), COPY)
            words = picked[t][:].bitcast(F32)
            for u in range(2):
                nc.tensor.transpose(turn_bank[t][:, u, :], words[:, u : 2 * P : 2], identity[:])

        def quantise_values(t):
            move_words = nc.vector.tensor_copy if t < 2 else nc.scalar.copy
            move_words(
                value_bf[t][:].bitcast(F32).rearrange("p (n u) -> p n u", u=2),
                turn_bank[t][:].rearrange("p u n -> p n u"),
            )
            nc.vector.quantize_mx(out=value_codes[t][:].bitcast(FP8X4), scales=value_scales[t][:], in_=value_bf[t][:])

        middle_keys(0)
        nc.vector.quantize_mx(
            out=query_codes[:].bitcast(FP8X4), scales=query_scales[:], in_=query_bf[:].rearrange("p w t -> p (w t)")
        )
        quantise_keys(0)
        score(0, 0)
        score(0, 1)
        pick_and_turn(0)
        middle_keys(1)
        quantise_keys(1)
        score(1, 0)
        quantise_values(0)
        score(1, 1)
        for t in range(1, PACK):
            pick_and_turn(t)

        halves = [slice(h * HALF_Q, (h + 1) * HALF_Q) for h in range(2)]
        weight_bf = [
            sb.tile([P, HALF_Q, PACK], BF16, name="weight_bf0", align_bytes=64),
            reused.tile([P, HALF_Q, PACK], BF16, name="weight_bf1", offset=spare, align_bytes=64),
        ]
        weight_codes = sb.tile([P, Q], U32, name="weight_codes", align_bytes=64)
        weight_scales = sb.tile([P, Q], U8, name="weight_scales", align_bytes=64)
        for h in range(2):
            nc.vector.scalar_tensor_tensor(
                out=weight_bf[h][:],
                in0=score_bank[h][:].rearrange("p r q -> p q r"),
                scalar=0.0,
                in1=factor[:].unsqueeze(1).to_broadcast([P, HALF_Q, PACK]),
                op0=ALU.max,
                op1=ALU.mult,
            )
        for h in range(2):
            nc.vector.quantize_mx(
                out=weight_codes[:, halves[h]].bitcast(FP8X4),
                scales=weight_scales[:, halves[h]],
                in_=weight_bf[h][:].rearrange("p q r -> p (q r)"),
            )

        sum_bank = [
            psum.tile([P, Q], F32, name="sum_bank%d" % t, tag=tag)
            for t, tag in enumerate(("turn2", "turn3", "score0", "score1"))
        ]
        sums = [sb.tile([P, Q], F32, name="sums%d" % t) for t in range(PACK)]

        def add_up(t):
            nc.tensor.matmul_mx(
                out=sum_bank[t][:],
                lhsT=value_codes[t][:].bitcast(FP8X4),
                lhsT_scale=value_scales[t][:],
                rhs=weight_codes[:].bitcast(FP8X4),
                rhs_scale=weight_scales[:],
                start=True,
                stop=True,
            )
            nc.scalar.copy(sums[t][:], sum_bank[t][:])

        for t in range(1, PACK):
            quantise_values(t)
        for t in range(PACK):
            add_up(t)

        half_lists = [list_q[:, h * HALF_Q // 16 : (h + 1) * HALF_Q // 16] for h in range(2)]
        out_rows = out_0.rearrange("(p t) q -> p t q", t=PACK)
        result = sb.tile([P, PACK, Q], F32, name="result")
        taken = [sb.tile([P, Q], F32, name="taken%d" % t, tag="taken", bufs=2) for t in range(PACK)]

        def take_off(t):
            for rows in halves if t == PACK - 1 else [slice(0, Q)]:
                nc.vector.tensor_tensor(result[:, t, rows], sums[t][:, rows], taken[t][:, rows], ALU.subtract)
            nc.sync.dma_start(out_rows[:, t, :], result[:, t, :])

        for t in (0, 1):
            for h in range(2):
                nc.vector.tensor_tensor(
                    taken[t][:, halves[h]], sums[t][:].indirect(half_lists[h]), hold_rows[:, halves[h]], ALU.mult
                )
        for t in (0, 1):
            take_off(t)
        for t in (2, 3):
            named = sb.tile([P, Q], F32, name="named%d" % t)
            for h in range(2):
                nc.scalar.activation(named[:, halves[h]], sums[t][:].indirect(half_lists[h]), COPY)
            nc.vector.tensor_tensor(taken[t][:], named[:], hold_rows[:], ALU.mult)
        for t in (2, 3):
            take_off(t)

        result_bf = sb.tile([P, Q, PACK], BF16, name="result_bf", align_bytes=64)
        result_codes = sb.tile([P, Q], U32, name="result_codes", align_bytes=64)
        result_scales = sb.tile([P, Q], U8, name="result_scales", align_bytes=64)
        for rows in halves:
            nc.vector.tensor_copy(
                result_bf[:, rows, :].rearrange("p (c i) t -> p c t i", i=4),
                result[:, :, rows].rearrange("p t (c i) -> p c t i", i=4),
            )
        out_words = out_1[0].rearrange("p c r -> p (c r)").bitcast(I32)
        for rows in halves:
            nc.vector.quantize_mx(
                out=result_codes[:, rows].bitcast(FP8X4),
                scales=result_scales[:, rows],
                in_=result_bf[:, rows, :].rearrange("p w t -> p (w t)"),
            )
            nc.sync.dma_start(out_words[:, rows], result_codes[:, rows].bitcast(I32))
        for g in range(4):
            queue = nc.sync if g % 2 else nc.scalar
            queue.dma_start(out_2[0, 4 * g : 4 * g + 4, :].bitcast(I32), result_scales[32 * g : 32 * g + 4, :].bitcast(I32))
